import numpy as np
import ml_dtypes


def mxq(x, axis, fmt="e4m3"):
    dtype, down = {"e4m3": (ml_dtypes.float8_e4m3fn, 7), "e5m2": (ml_dtypes.float8_e5m2, 14)}[fmt]
    v = np.moveaxis(np.asarray(x, np.float32).astype(ml_dtypes.bfloat16).astype(np.float64), axis, -1)
    blocks = v.reshape(v.shape[:-1] + (-1, 32))
    amax = np.abs(blocks).max(-1, keepdims=True)
    byte = np.maximum(np.where(amax > 0, np.frexp(amax)[1] - 1 + 127, 0) - down, 1)
    scale = np.exp2(byte - 127.0)
    codes = (blocks / scale).astype(np.float32).astype(dtype).astype(np.float64)
    return np.moveaxis((codes * scale).reshape(v.shape), -1, axis)


WIDE = False


def mx_kscale(k):
    if not WIDE:
        return np.ones(k)
    levels = np.array([10, -10, 5, -5, 0])
    if k % 512:
        return np.exp2(np.random.permutation(np.resize(levels, k // 32))).repeat(32)
    a = np.empty((k // 512, 16))
    for p in range(k // 512):
        a[p, :8] = np.random.permutation(np.resize(levels, 8))
        for g in range(8):
            far = levels[np.abs(levels - a[p, g]) >= 10]
            a[p, g + 8] = far[np.random.randint(len(far))]
    return np.exp2(a.ravel()).repeat(32)


def f64(x):
    return np.asarray(x).astype(np.float64)


def striped(idx):
    return np.tile(idx.reshape(-1, 16).T, (8, 1)).astype(np.uint16)


def unstriped(offs):
    return offs[:16].T.reshape(-1).astype(np.int64)


E2M1 = np.array([0.0, 0.5, 1.0, 1.5, 2.0, 3.0, 4.0, 6.0, -0.0, -0.5, -1.0, -1.5, -2.0, -3.0, -4.0, -6.0])


def pack_weight(w, fmt):
    k, n = w.shape
    w = f64(np.asarray(w, np.float32).astype(ml_dtypes.bfloat16)).reshape(k // 32, 32, n)
    amax = np.abs(w).max(1)
    if fmt == "e4m3":
        byte = np.frexp(amax)[1] - 1 + 127 - 7
    else:
        mant, ex = np.frexp(amax / 6.0)
        byte = np.where(mant > 0.5, ex, ex - 1) + 127
    byte = np.clip(np.where(amax > 0, byte, 1), 1, 254)
    scaled = (w * np.exp2(127.0 - byte)[:, None, :]).reshape(k, n).astype(np.float32)
    by_word = np.ascontiguousarray(scaled.reshape(k // 512, 128, 4, n).transpose(0, 1, 3, 2))
    if fmt == "e4m3":
        words = by_word.astype(ml_dtypes.float8_e4m3fn).view(np.uint8)
    else:
        c = by_word.astype(ml_dtypes.float4_e2m1fn).view(np.uint8) & 0xF
        words = (c[..., 0::2] | (c[..., 1::2] << 4)).reshape(k // 512, 128, 2 * n)
    return np.ascontiguousarray(words), np.ascontiguousarray(byte.astype(np.uint8).reshape(k // 512, 16, n))


def unpack_weight(words, scales, fmt):
    g, _, n = scales.shape
    words = np.ascontiguousarray(words).reshape(g, 128, n, -1)
    if fmt == "e4m3":
        vals = words.view(ml_dtypes.float8_e4m3fn).astype(np.float64)
    else:
        nib = np.empty((g, 128, n, 4), np.uint8)
        nib[..., 0::2] = words & 0xF
        nib[..., 1::2] = words >> 4
        vals = E2M1[nib]
    vals = vals * np.repeat(np.exp2(scales.astype(np.float64) - 127.0), 8, axis=1)[..., None]
    return vals.transpose(0, 1, 3, 2).reshape(g * 512, n)


def gelu(v):
    return 0.5 * v * (1.0 + np.tanh(np.sqrt(2.0 / np.pi) * (v + 0.044715 * v**3)))


def bf(x):
    return np.asarray(x, np.float32).astype(ml_dtypes.bfloat16)

def planes(Y):
    n, m = Y.shape
    b = f64(bf(Y)).reshape(n // 32, 32, m)
    amax = np.abs(b).max(1)
    byte = np.clip(np.where(amax > 0, np.frexp(amax)[1] - 1 + 127 - 7, 1), 1, 254)
    codes = (b * np.exp2(127.0 - byte)[:, None, :]).reshape(n, m).astype(np.float32).astype(ml_dtypes.float8_e4m3fn).view(np.uint8)
    words = codes.reshape(n // 512, 128, 4, m).transpose(0, 1, 3, 2)
    return np.ascontiguousarray(words), np.ascontiguousarray(byte.astype(np.uint8).reshape(n // 512, 16, m))


K, K2, T, T2, S, H, N = 1024, 512, 2048, 2048, 1024, 1024, 1024


def setup_inputs():
    n = np.random.standard_normal
    s = mx_kscale(K)[:, None]
    s2 = mx_kscale(K2)[:, None]
    u = mx_kscale(H)[:, None]
    tab_words, tab_scales = pack_weight(n((K, T)) * s, "e4m3")
    tab2_words, tab2_scales = pack_weight(n((K2, T2)) * s2, "e4m3")
    wa_words, wa_scales = pack_weight(0.8 * n((K, H)) / np.sqrt(K) / s, "e2m1")
    wb = (0.8 * n((K2, H)) / np.sqrt(K2) / s2).astype(np.float32)
    wr = 0.7 * n((H, N)) / np.sqrt(H) * np.exp(0.8 * n(N)) / u
    wr_words, wr_scales = pack_weight(wr, "e4m3")
    return {
        "tab_words": tab_words, "tab_scales": tab_scales,
        "tab2_words": tab2_words, "tab2_scales": tab2_scales,
        "offs": striped(np.random.permutation(T)[:S]),
        "offs2": striped(np.random.permutation(T2)[:S]),
        "gT": np.exp(0.5 * n((H, T))).astype(np.float32),
        "wa_words": wa_words, "wa_scales": wa_scales, "wb": wb,
        "amp": (np.exp(0.3 * n(H)) * u[:, 0]).astype(np.float32),
        "wr_words": wr_words, "wr_scales": wr_scales,
    }


def reference(tab_words, tab_scales, tab2_words, tab2_scales, offs, offs2, gT, wa_words, wa_scales, wb, amp, wr_words, wr_scales):
    v = unpack_weight(tab_words, tab_scales, "e4m3")[:, unstriped(offs)]
    v2 = unpack_weight(tab2_words, tab2_scales, "e4m3")[:, unstriped(offs2)]
    g = f64(gT)[:, unstriped(offs)]
    a = unpack_weight(wa_words, wa_scales, "e2m1").T @ v
    b = mxq(f64(wb), 0, "e4m3").T @ v2
    h = f64(amp)[:, None] * np.sqrt(g + np.square(a - b))
    y = unpack_weight(wr_words, wr_scales, "e4m3").T @ mxq(h, 0, "e4m3")
    words, scales = planes(y)
    return y, words, scales

@@ -1,0 +1,300 @@
+from contextlib import ExitStack
+
+import concourse.mybir as mybir
+
+K, K2, T, S, H, N = 1024, 512, 2048, 1024, 1024, 1024
+FLOPS = 2 * S * (K * H + K2 * H + H * N)
+
+F32 = mybir.dt.float32
+BF16 = mybir.dt.bfloat16
+I32 = mybir.dt.int32
+U32 = mybir.dt.uint32
+U16 = mybir.dt.uint16
+U8 = mybir.dt.uint8
+FP8X4 = mybir.dt.float8_e4m3fn_x4
+FP4X4 = mybir.dt.float4_e2m1fn_x4
+ACT = mybir.ActivationFunctionType
+ALU = mybir.AluOpType
+
+P = 128
+PACK = 4
+GROUP = P * PACK
+HALF = 512
+CHUNK = 256
+YCOLS = 128
+AL = 64
+
+
+def tile_list_multiquadric_deform_kernel(
+    tc, tab_words, tab_scales, tab2_words, tab2_scales, offs, offs2, gT,
+    wa_words, wa_scales, wb, amp, wr_words, wr_scales, out_0, out_1, out_2,
+):
+    nc = tc.nc
+    with ExitStack() as ctx:
+        keep = ctx.enter_context(tc.tile_pool(name="keep", bufs=1))
+        g_pool = ctx.enter_context(tc.tile_pool(name="g_rows", bufs=6))
+        stage = ctx.enter_context(tc.tile_pool(name="stage", bufs=3))
+        rounded = ctx.enter_context(tc.tile_pool(name="rounded", bufs=2))
+        y_rounded = ctx.enter_context(tc.tile_pool(name="y_rounded", bufs=4))
+        d_psum = ctx.enter_context(tc.psum_pool(name="d_psum", bufs=4))
+        y_psum = ctx.enter_context(tc.psum_pool(name="y_psum", bufs=4))
+
+        def held(name, shape, dtype):
+            return keep.tile(shape, dtype, name=name, align_bytes=AL)
+
+        idx = keep.tile([P, S // 16], U16, name="idx")
+        idx2 = keep.tile([P, S // 16], U16, name="idx2")
+        tab_w = [held("tab_w%d" % a, [P, T], U32) for a in range(2)]
+        tab2_w = held("tab2_w", [P, T], U32)
+        tab_s = held("tab_s", [P, T], U8)
+        tab2_s = held("tab2_s", [P, T], U8)
+        w_s_raw = held("w_s_raw", [P, H], U8)
+        v_s1 = held("v_s1", [P, S], U8)
+        wa_s1 = held("wa_s1", [P, H], U8)
+        for plane in (tab_s, w_s_raw, tab2_s, v_s1, wa_s1):
+            nc.vector.memset(plane[:].bitcast(I32), 0)
+
+        def load_scale_rows(queue, plane, first_row, scales):
+            passes = scales.shape[0]
+            for q in range(4):
+                row = 32 * q + first_row
+                queue.dma_start(
+                    out=plane[row : row + 4 * passes, :].bitcast(I32),
+                    in_=scales[:, 4 * q : 4 * q + 4, :].bitcast(I32),
+                )
+
+        nc.sync.dma_start(idx[:], offs)
+        nc.sync.dma_start(idx2[:], offs2)
+
+        def load_words(tile, words):
+            nc.sync.dma_start(
+                out=tile[:].bitcast(I32), in_=words.rearrange("p n i -> p (n i)").bitcast(I32)
+            )
+
+        load_words(tab_w[0], tab_words[0])
+        load_scale_rows(nc.sync, tab_s, 0, tab_scales)
+        load_words(tab_w[1], tab_words[1])
+        load_scale_rows(nc.sync, w_s_raw, 0, wa_scales)
+        load_scale_rows(nc.gpsimd, w_s_raw, 8, wr_scales)
+        load_words(tab2_w, tab2_words[0])
+        load_scale_rows(nc.sync, tab2_s, 0, tab2_scales)
+
+        def deal_columns(copy, dealt, raw):
+            copy(
+                out=dealt.rearrange("p (b t m) -> p b m t", t=PACK, m=P),
+                in_=raw.rearrange("p (b m t) -> p b m t", t=PACK, m=P),
+            )
+
+        def list_cols(tile, first, count):
+            return tile[:, first // 16 : (first + count) // 16]
+
+        v_s = held("v_s", [P, S], U8)
+        nc.vector.tensor_copy(v_s[:], tab_s[:].indirect(idx[:]))
+        nc.sync.dma_start(out=v_s1[0:112, :].bitcast(I32), in_=v_s[4:116, :].bitcast(I32))
+
+        w_s = held("w_s", [P, H], U8)
+        deal_columns(nc.vector.tensor_copy, w_s[:], w_s_raw[:])
+        nc.sync.dma_start(out=wa_s1[0:112, :].bitcast(I32), in_=w_s[4:116, :].bitcast(I32))
+
+        wa_raw = held("wa_raw", [P, 2, H], U16)
+        nc.sync.dma_start(
+            out=wa_raw[:].bitcast(I32),
+            in_=wa_words.rearrange("a p n -> p a n").bitcast(I32),
+        )
+
+        wb_rows = wb.rearrange("(p i) r -> p i r", i=PACK)
+        g_rows = gT.rearrange("(b p t) n -> b t p n", p=P, t=PACK)
+        wb_raw = {}
+        g_tab = {}
+
+        def load_wb(b):
+            wb_raw[b] = stage.tile([P, PACK, GROUP], F32, name="wb_raw%d" % b, tag="stage", align_bytes=AL)
+            nc.sync.dma_start(out=wb_raw[b][:], in_=wb_rows[:, :, b * GROUP : (b + 1) * GROUP])
+
+        def load_g(b, t):
+            g_tab[b, t] = g_pool.tile([P, T], F32, name="g_tab%d%d" % (b, t), tag="g_tab", align_bytes=AL)
+            nc.sync.dma_start(out=g_tab[b, t][:], in_=g_rows[b, t])
+
+        load_wb(0)
+        amp_sb = held("amp_sb", [P, 2, PACK], F32)
+        nc.sync.dma_start(out=amp_sb[:], in_=amp.rearrange("(b p t) -> p b t", p=P, t=PACK))
+        load_g(0, 0)
+        load_wb(1)
+        for t in range(1, PACK):
+            load_g(0, t)
+        wr_raw = held("wr_raw", [P, 2, N], U32)
+        nc.sync.dma_start(
+            out=wr_raw[:].bitcast(I32),
+            in_=wr_words.rearrange("a p n i -> p a (n i)").bitcast(I32),
+        )
+        for t in range(PACK):
+            load_g(1, t)
+
+        wa_w = held("wa_w", [P, 2, H], U16)
+        for a in range(2):
+            deal_columns(nc.scalar.copy, wa_w[:, a, :], wa_raw[:, a, :])
+
+        wb_w = held("wb_w", [P, H], U32)
+        wb_s = held("wb_s", [P, H], U8)
+
+        def quantise_wb(b):
+            wb_bf = rounded.tile([P, GROUP, PACK], BF16, name="wb_bf%d" % b, tag="wb_bf", align_bytes=AL)
+            nc.scalar.activation(
+                out=wb_bf[:].rearrange("p (t m) i -> p m i t", t=PACK),
+                in_=wb_raw[b][:].rearrange("p i (m t) -> p m i t", t=PACK),
+                func=ACT.Copy,
+                scale=-1.0,
+            )
+            cols = slice(b * GROUP, (b + 1) * GROUP)
+            nc.vector.quantize_mx(
+                out=wb_w[:, cols].bitcast(FP8X4), scales=wb_s[:, cols],
+                in_=wb_bf[:].rearrange("p n i -> p (n i)"),
+            )
+
+        quantise_wb(0)
+        amp_sq = held("amp_sq", [P, 2, PACK], F32)
+        nc.vector.tensor_tensor(out=amp_sq[:], in0=amp_sb[:], in1=amp_sb[:], op=ALU.mult)
+
+        v_w = {}
+        v2_w = {}
+        v2_s = {}
+        for half in range(2):
+            for a in range(2):
+                v_w[a, half] = held("v_w%d%d" % (a, half), [P, HALF], U32)
+                nc.vector.tensor_copy(v_w[a, half][:], tab_w[a][:].indirect(list_cols(idx, half * HALF, HALF)))
+            v2_w[half] = held("v2_w%d" % half, [P, HALF], U32)
+            nc.vector.tensor_copy(v2_w[half][:], tab2_w[:].indirect(list_cols(idx2, half * HALF, HALF)))
+            v2_s[half] = held("v2_s%d" % half, [P, HALF], U8)
+            nc.vector.tensor_copy(v2_s[half][:], tab2_s[:].indirect(list_cols(idx2, half * HALF, HALF)))
+
+        width = {0: HALF, 1: CHUNK}
+        x = {}
+        for b in range(2):
+            for first in range(0, S, width[b]):
+                x[b, first] = held("x%d_%d" % (b, first), [P, PACK, width[b]], F32)
+
+        def squared_separation(b, t, half):
+            rows = slice(b * GROUP + t * P, b * GROUP + (t + 1) * P)
+            cols = slice(half * HALF, (half + 1) * HALF)
+            d = d_psum.tile([P, HALF], F32, name="d", tag="d")
+            nc.tensor.matmul_mx(
+                out=d[:], lhsT=wa_w[:, 0, rows].bitcast(FP4X4), lhsT_scale=w_s[:, rows],
+                rhs=v_w[0, half][:].bitcast(FP8X4), rhs_scale=v_s[:, cols], start=True, stop=False,
+            )
+            nc.tensor.matmul_mx(
+                out=d[:], lhsT=wb_w[:, rows].bitcast(FP8X4), lhsT_scale=wb_s[:, rows],
+                rhs=v2_w[half][:].bitcast(FP8X4), rhs_scale=v2_s[half][:], start=False, stop=False,
+            )
+            nc.tensor.matmul_mx(
+                out=d[:], lhsT=wa_w[:, 1, rows].bitcast(FP4X4), lhsT_scale=wa_s1[:, rows],
+                rhs=v_w[1, half][:].bitcast(FP8X4), rhs_scale=v_s1[:, cols], start=False, stop=True,
+            )
+            for part in range(0, HALF, width[b]):
+                nc.scalar.activation(
+                    out=x[b, half * HALF + part][:, t, :], in_=d[:, part : part + width[b]],
+                    func=ACT.Square, scale=amp_sb[:, b, t : t + 1],
+                )
+
+        g_picked = [held("g_picked%d" % i, [P, S], F32) for i in range(2)]
+
+        def add_shape(b, t, first, picked):
+            nc.vector.scalar_tensor_tensor(
+                out=x[b, first][:, t, :], in0=picked, scalar=amp_sq[:, b, t : t + 1],
+                in1=x[b, first][:, t, :], op0=ALU.mult, op1=ALU.add,
+            )
+
+        h_w = [held("h_w%d" % b, [P, S], U32) for b in range(2)]
+        h_s = [held("h_s%d" % b, [P, S], U8) for b in range(2)]
+
+        def quantise_h(b, first):
+            n = width[b]
+            h_bf = rounded.tile([P, n, PACK], BF16, name="h_bf", tag="h_bf", align_bytes=AL)
+            nc.scalar.activation(
+                out=h_bf[:].rearrange("p (c i) t -> p c t i", i=4),
+                in_=x[b, first][:].rearrange("p t (c i) -> p c t i", i=4),
+                func=ACT.Sqrt,
+            )
+            cols = slice(first, first + n)
+            nc.vector.quantize_mx(
+                out=h_w[b][:, cols].bitcast(FP8X4), scales=h_s[b][:, cols],
+                in_=h_bf[:].rearrange("p n t -> p (n t)"),
+            )
+
+        for half in range(2):
+            for t in range(PACK):
+                squared_separation(0, t, half)
+        quantise_wb(1)
+        for t in range(PACK):
+            picked = g_picked[t % 2]
+            nc.vector.tensor_copy(picked[:], g_tab[0, t][:].indirect(idx[:]))
+            for first in range(0, S, HALF):
+                add_shape(0, t, first, picked[:, first : first + HALF])
+        for first in range(0, S, HALF):
+            quantise_h(0, first)
+        for half in range(2):
+            for t in range(PACK):
+                squared_separation(1, t, half)
+
+        wr_w = held("wr_w", [P, 2, N], U32)
+        for a in range(2):
+            deal_columns(nc.scalar.copy, wr_w[:, a, :], wr_raw[:, a, :])
+
+        y_w = [held("y_w%d" % g, [P, S], U32) for g in range(2)]
+        y_s = held("y_s", [P, S], U8)
+        out_rows = out_0.rearrange("(g p t) j -> g p t j", p=P, t=PACK)
+
+        def make_h(first):
+            for t in range(PACK):
+                picked = g_picked[(first // CHUNK) % 2][:, t * CHUNK : (t + 1) * CHUNK]
+                nc.vector.tensor_copy(picked, g_tab[1, t][:].indirect(list_cols(idx, first, CHUNK)))
+                add_shape(1, t, first, picked)
+            quantise_h(1, first)
+
+        def make_y(first):
+            cols = slice(first, first + CHUNK)
+            y = stage.tile([P, 2, PACK, CHUNK], F32, name="y", tag="stage", align_bytes=AL)
+            for g in range(2):
+                y_bf = y_rounded.tile([P, CHUNK, PACK], BF16, name="y_bf", tag="y_bf", align_bytes=AL)
+                for part in range(0, CHUNK, YCOLS):
+                    moving = slice(first + part, first + part + YCOLS)
+                    acc = y_psum.tile([P, PACK, YCOLS], F32, name="acc", tag="acc")
+                    for t in range(PACK):
+                        rows = slice(g * GROUP + t * P, g * GROUP + (t + 1) * P)
+                        for b in range(2):
+                            nc.tensor.matmul_mx(
+                                out=acc[:, t, :], lhsT=wr_w[:, b, rows].bitcast(FP8X4),
+                                lhsT_scale=w_s[8 + 4 * b : P, rows],
+                                rhs=h_w[b][:, moving].bitcast(FP8X4), rhs_scale=h_s[b][:, moving],
+                                start=(b == 0), stop=(b == 1),
+                            )
+                    nc.scalar.copy(out=y[:, g, :, part : part + YCOLS], in_=acc[:])
+                    if first == 0:
+                        nc.scalar.copy(
+                            out=y_bf[:, part : part + YCOLS, :], in_=acc[:].rearrange("p t j -> p j t")
+                        )
+                if first > 0:
+                    nc.vector.tensor_copy(
+                        out=y_bf[:].rearrange("p (c i) t -> p c t i", i=4),
+                        in_=y[:, g].rearrange("p t (c i) -> p c t i", i=4),
+                    )
+                nc.sync.dma_start(out=out_rows[g][:, :, cols], in_=y[:, g])
+                nc.vector.quantize_mx(
+                    out=y_w[g][:, cols].bitcast(FP8X4), scales=y_s[4 * g : P, cols],
+                    in_=y_bf[:].rearrange("p n t -> p (n t)"),
+                )
+                nc.sync.dma_start(
+                    out=out_1[g].rearrange("p n i -> p (n i)").bitcast(I32)[:, cols],
+                    in_=y_w[g][:, cols].bitcast(I32),
+                )
+
+        make_h(0)
+        for first in range(0, S, CHUNK):
+            if first + CHUNK < S:
+                make_h(first + CHUNK)
+            make_y(first)
+
+        for q in range(4):
+            nc.sync.dma_start(
+                out=out_2[:, 4 * q : 4 * q + 4, :].bitcast(I32),
+                in_=y_s[32 * q : 32 * q + 8, :].bitcast(I32),
+            )

@@ -34,10 +34,8 @@ def tile_list_multiquadric_deform_kernel(
         keep = ctx.enter_context(tc.tile_pool(name="keep", bufs=1))
         g_pool = ctx.enter_context(tc.tile_pool(name="g_rows", bufs=6))
         stage = ctx.enter_context(tc.tile_pool(name="stage", bufs=3))
-        rounded = ctx.enter_context(tc.tile_pool(name="rounded", bufs=2))
         y_rounded = ctx.enter_context(tc.tile_pool(name="y_rounded", bufs=4))
-        d_psum = ctx.enter_context(tc.psum_pool(name="d_psum", bufs=4))
-        y_psum = ctx.enter_context(tc.psum_pool(name="y_psum", bufs=4))
+        psum = ctx.enter_context(tc.psum_pool(name="psum", bufs=8))
 
         def held(name, shape, dtype):
             return keep.tile(shape, dtype, name=name, align_bytes=AL)
@@ -48,36 +46,26 @@ def tile_list_multiquadric_deform_kernel(
         tab2_w = held("tab2_w", [P, T], U32)
         tab_s = held("tab_s", [P, T], U8)
         tab2_s = held("tab2_s", [P, T], U8)
-        w_s_raw = held("w_s_raw", [P, H], U8)
+        wa_s_raw = held("wa_s_raw", [P, 2, H], U8)
+        wr_s_raw = held("wr_s_raw", [P, N], U8)
         v_s1 = held("v_s1", [P, S], U8)
-        wa_s1 = held("wa_s1", [P, H], U8)
-        for plane in (tab_s, w_s_raw, tab2_s, v_s1, wa_s1):
+        for plane in (tab_s, tab2_s):
+            nc.gpsimd.memset(plane[:].bitcast(I32), 0)
+        for plane in (wa_s_raw, v_s1, wr_s_raw):
             nc.vector.memset(plane[:].bitcast(I32), 0)
 
-        def load_scale_rows(queue, plane, first_row, scales):
+        def load_scale_rows(queue, plane, scales):
             passes = scales.shape[0]
             for q in range(4):
-                row = 32 * q + first_row
                 queue.dma_start(
-                    out=plane[row : row + 4 * passes, :].bitcast(I32),
+                    out=plane[32 * q : 32 * q + 4 * passes, :].bitcast(I32),
                     in_=scales[:, 4 * q : 4 * q + 4, :].bitcast(I32),
                 )
-
-        nc.sync.dma_start(idx[:], offs)
-        nc.sync.dma_start(idx2[:], offs2)
 
         def load_words(tile, words):
             nc.sync.dma_start(
                 out=tile[:].bitcast(I32), in_=words.rearrange("p n i -> p (n i)").bitcast(I32)
             )
-
-        load_words(tab_w[0], tab_words[0])
-        load_scale_rows(nc.sync, tab_s, 0, tab_scales)
-        load_words(tab_w[1], tab_words[1])
-        load_scale_rows(nc.sync, w_s_raw, 0, wa_scales)
-        load_scale_rows(nc.gpsimd, w_s_raw, 8, wr_scales)
-        load_words(tab2_w, tab2_words[0])
-        load_scale_rows(nc.sync, tab2_s, 0, tab2_scales)
 
         def deal_columns(copy, dealt, raw):
             copy(
@@ -85,22 +73,8 @@ def tile_list_multiquadric_deform_kernel(
                 in_=raw.rearrange("p (b m t) -> p b m t", t=PACK, m=P),
             )
 
-        def list_cols(tile, first, count):
-            return tile[:, first // 16 : (first + count) // 16]
-
-        v_s = held("v_s", [P, S], U8)
-        nc.vector.tensor_copy(v_s[:], tab_s[:].indirect(idx[:]))
-        nc.sync.dma_start(out=v_s1[0:112, :].bitcast(I32), in_=v_s[4:116, :].bitcast(I32))
-
-        w_s = held("w_s", [P, H], U8)
-        deal_columns(nc.vector.tensor_copy, w_s[:], w_s_raw[:])
-        nc.sync.dma_start(out=wa_s1[0:112, :].bitcast(I32), in_=w_s[4:116, :].bitcast(I32))
-
-        wa_raw = held("wa_raw", [P, 2, H], U16)
-        nc.sync.dma_start(
-            out=wa_raw[:].bitcast(I32),
-            in_=wa_words.rearrange("a p n -> p a n").bitcast(I32),
-        )
+        def shift_planes(second, both):
+            nc.sync.dma_start(out=second[0:112, :].bitcast(I32), in_=both[4:116, :].bitcast(I32))
 
         wb_rows = wb.rearrange("(p i) r -> p i r", i=PACK)
         g_rows = gT.rearrange("(b p t) n -> b t p n", p=P, t=PACK)
@@ -115,140 +89,173 @@ def tile_list_multiquadric_deform_kernel(
             g_tab[b, t] = g_pool.tile([P, T], F32, name="g_tab%d%d" % (b, t), tag="g_tab", align_bytes=AL)
             nc.sync.dma_start(out=g_tab[b, t][:], in_=g_rows[b, t])
 
-        load_wb(0)
+        nc.sync.dma_start(idx[:], offs)
+        nc.sync.dma_start(idx2[:], offs2)
         amp_sb = held("amp_sb", [P, 2, PACK], F32)
         nc.sync.dma_start(out=amp_sb[:], in_=amp.rearrange("(b p t) -> p b t", p=P, t=PACK))
-        load_g(0, 0)
+        load_scale_rows(nc.sync, tab_s, tab_scales)
+        load_words(tab_w[0], tab_words[0])
+        load_words(tab_w[1], tab_words[1])
+        load_scale_rows(nc.sync, tab2_s, tab2_scales)
+        load_words(tab2_w, tab2_words[0])
+        wa_raw = held("wa_raw", [P, 2, H], U16)
+        nc.sync.dma_start(
+            out=wa_raw[:].bitcast(I32),
+            in_=wa_words.rearrange("a p n -> p a n").bitcast(I32),
+        )
+        for q in range(4):
+            nc.sync.dma_start(
+                out=wa_s_raw[32 * q : 32 * q + 4].bitcast(I32),
+                in_=wa_scales[:, 4 * q : 4 * q + 4, :].rearrange("a r n -> r a n").bitcast(I32),
+            )
+
+        v_s = held("v_s", [P, S], U8)
+        nc.vector.tensor_copy(v_s[:], tab_s[:].indirect(idx[:]))
+        shift_planes(v_s1, v_s)
+        load_wb(0)
         load_wb(1)
-        for t in range(1, PACK):
-            load_g(0, t)
+        load_g(0, 0)
+        load_g(0, 1)
         wr_raw = held("wr_raw", [P, 2, N], U32)
         nc.sync.dma_start(
             out=wr_raw[:].bitcast(I32),
             in_=wr_words.rearrange("a p n i -> p a (n i)").bitcast(I32),
         )
+        load_g(0, 2)
+        load_scale_rows(nc.sync, wr_s_raw, wr_scales)
+        load_g(0, 3)
         for t in range(PACK):
             load_g(1, t)
+
+        def list_cols(tile, first, count):
+            return tile[:, first // 16 : (first + count) // 16]
+
+        g_picked = [held("g_picked%d" % i, [P, S], F32) for i in range(2)]
 
         wa_w = held("wa_w", [P, 2, H], U16)
         for a in range(2):
             deal_columns(nc.scalar.copy, wa_w[:, a, :], wa_raw[:, a, :])
 
-        wb_w = held("wb_w", [P, H], U32)
-        wb_s = held("wb_s", [P, H], U8)
+        wb_w = [held("wb_w%d" % b, [P, GROUP], U32) for b in range(2)]
+        wb_s = [held("wb_s%d" % b, [P, GROUP], U8) for b in range(2)]
+        half_picked = [held("half_picked%d" % i, [P, HALF], F32) for i in range(3)]
 
-        def quantise_wb(b):
-            wb_bf = rounded.tile([P, GROUP, PACK], BF16, name="wb_bf%d" % b, tag="wb_bf", align_bytes=AL)
+        def quantise_wb(b, buffer):
+            wb_bf = buffer[:].bitcast(BF16)
             nc.scalar.activation(
-                out=wb_bf[:].rearrange("p (t m) i -> p m i t", t=PACK),
+                out=wb_bf.rearrange("p (t m i) -> p m i t", t=PACK, i=PACK),
                 in_=wb_raw[b][:].rearrange("p i (m t) -> p m i t", t=PACK),
                 func=ACT.Copy,
                 scale=-1.0,
             )
-            cols = slice(b * GROUP, (b + 1) * GROUP)
-            nc.vector.quantize_mx(
-                out=wb_w[:, cols].bitcast(FP8X4), scales=wb_s[:, cols],
-                in_=wb_bf[:].rearrange("p n i -> p (n i)"),
-            )
+            nc.vector.quantize_mx(out=wb_w[b][:].bitcast(FP8X4), scales=wb_s[b][:], in_=wb_bf)
 
-        quantise_wb(0)
+        for b in range(2):
+            quantise_wb(b, g_picked[1 - b])
         amp_sq = held("amp_sq", [P, 2, PACK], F32)
         nc.vector.tensor_tensor(out=amp_sq[:], in0=amp_sb[:], in1=amp_sb[:], op=ALU.mult)
 
-        v_w = {}
-        v2_w = {}
-        v2_s = {}
-        for half in range(2):
-            for a in range(2):
-                v_w[a, half] = held("v_w%d%d" % (a, half), [P, HALF], U32)
-                nc.vector.tensor_copy(v_w[a, half][:], tab_w[a][:].indirect(list_cols(idx, half * HALF, HALF)))
-            v2_w[half] = held("v2_w%d" % half, [P, HALF], U32)
-            nc.vector.tensor_copy(v2_w[half][:], tab2_w[:].indirect(list_cols(idx2, half * HALF, HALF)))
-            v2_s[half] = held("v2_s%d" % half, [P, HALF], U8)
-            nc.vector.tensor_copy(v2_s[half][:], tab2_s[:].indirect(list_cols(idx2, half * HALF, HALF)))
+        v_w = [held("v_w%d" % a, [P, S], U32) for a in range(2)]
+        v2_w = held("v2_w", [P, S], U32)
+        v2_s = held("v2_s", [P, S], U8)
+        for a in range(2):
+            nc.vector.tensor_copy(v_w[a][:], tab_w[a][:].indirect(idx[:]))
+        nc.vector.tensor_copy(v2_s[:], tab2_s[:].indirect(idx2[:]))
+        nc.vector.tensor_copy(v2_w[:], tab2_w[:].indirect(idx2[:]))
+        wa_s = held("wa_s", [P, 2, H], U8)
+        nc.vector.tensor_copy(
+            out=wa_s[:].rearrange("p a (b t m) -> p (a b) m t", t=PACK, m=P),
+            in_=wa_s_raw[:].rearrange("p a (b m t) -> p (a b) m t", t=PACK, m=P),
+        )
 
-        width = {0: HALF, 1: CHUNK}
+        width = {0: S, 1: HALF}
         x = {}
         for b in range(2):
             for first in range(0, S, width[b]):
                 x[b, first] = held("x%d_%d" % (b, first), [P, PACK, width[b]], F32)
 
+        def x_cols(b, first, count):
+            start = first - first % width[b]
+            return x[b, start][:, :, first - start : first - start + count]
+
         def squared_separation(b, t, half):
             rows = slice(b * GROUP + t * P, b * GROUP + (t + 1) * P)
             cols = slice(half * HALF, (half + 1) * HALF)
-            d = d_psum.tile([P, HALF], F32, name="d", tag="d")
+            d = psum.tile([P, HALF], F32, name="d", tag="bank")
             nc.tensor.matmul_mx(
-                out=d[:], lhsT=wa_w[:, 0, rows].bitcast(FP4X4), lhsT_scale=w_s[:, rows],
-                rhs=v_w[0, half][:].bitcast(FP8X4), rhs_scale=v_s[:, cols], start=True, stop=False,
+                out=d[:], lhsT=wa_w[:, 0, rows].bitcast(FP4X4), lhsT_scale=wa_s[:, 0, rows],
+                rhs=v_w[0][:, cols].bitcast(FP8X4), rhs_scale=v_s[:, cols], start=True, stop=False,
             )
             nc.tensor.matmul_mx(
-                out=d[:], lhsT=wb_w[:, rows].bitcast(FP8X4), lhsT_scale=wb_s[:, rows],
-                rhs=v2_w[half][:].bitcast(FP8X4), rhs_scale=v2_s[half][:], start=False, stop=False,
+                out=d[:], lhsT=wa_w[:, 1, rows].bitcast(FP4X4), lhsT_scale=wa_s[:, 1, rows],
+                rhs=v_w[1][:, cols].bitcast(FP8X4), rhs_scale=v_s1[:, cols], start=False, stop=False,
             )
             nc.tensor.matmul_mx(
-                out=d[:], lhsT=wa_w[:, 1, rows].bitcast(FP4X4), lhsT_scale=wa_s1[:, rows],
-                rhs=v_w[1, half][:].bitcast(FP8X4), rhs_scale=v_s1[:, cols], start=False, stop=True,
+                out=d[:], lhsT=wb_w[b][:, t * P : (t + 1) * P].bitcast(FP8X4), lhsT_scale=wb_s[b][:, t * P : (t + 1) * P],
+                rhs=v2_w[:, cols].bitcast(FP8X4), rhs_scale=v2_s[:, cols], start=False, stop=True,
             )
-            for part in range(0, HALF, width[b]):
+            step = min(HALF, width[b])
+            for part in range(0, HALF, step):
                 nc.scalar.activation(
-                    out=x[b, half * HALF + part][:, t, :], in_=d[:, part : part + width[b]],
+                    out=x_cols(b, half * HALF + part, step)[:, t, :], in_=d[:, part : part + step],
                     func=ACT.Square, scale=amp_sb[:, b, t : t + 1],
                 )
 
-        g_picked = [held("g_picked%d" % i, [P, S], F32) for i in range(2)]
-
-        def add_shape(b, t, first, picked):
+        def add_shape(b, t, first, count, picked):
+            squares = x_cols(b, first, count)[:, t, :]
             nc.vector.scalar_tensor_tensor(
-                out=x[b, first][:, t, :], in0=picked, scalar=amp_sq[:, b, t : t + 1],
-                in1=x[b, first][:, t, :], op0=ALU.mult, op1=ALU.add,
+                out=squares, in0=picked, scalar=amp_sq[:, b, t : t + 1],
+                in1=squares, op0=ALU.mult, op1=ALU.add,
             )
 
         h_w = [held("h_w%d" % b, [P, S], U32) for b in range(2)]
         h_s = [held("h_s%d" % b, [P, S], U8) for b in range(2)]
 
-        def quantise_h(b, first):
-            n = width[b]
-            h_bf = rounded.tile([P, n, PACK], BF16, name="h_bf", tag="h_bf", align_bytes=AL)
+        def quantise_h(b, first, n, buffer):
+            h_bf = buffer[:, : 2 * n].bitcast(BF16)
             nc.scalar.activation(
-                out=h_bf[:].rearrange("p (c i) t -> p c t i", i=4),
-                in_=x[b, first][:].rearrange("p t (c i) -> p c t i", i=4),
+                out=h_bf.rearrange("p (c i t) -> p c t i", i=4, t=PACK),
+                in_=x_cols(b, first, n).rearrange("p t (c i) -> p c t i", i=4),
                 func=ACT.Sqrt,
             )
             cols = slice(first, first + n)
             nc.vector.quantize_mx(
                 out=h_w[b][:, cols].bitcast(FP8X4), scales=h_s[b][:, cols],
-                in_=h_bf[:].rearrange("p n t -> p (n t)"),
+                in_=h_bf,
             )
 
-        for half in range(2):
-            for t in range(PACK):
+        for t in range(PACK - 1):
+            for half in range(2):
                 squared_separation(0, t, half)
-        quantise_wb(1)
         for t in range(PACK):
-            picked = g_picked[t % 2]
-            nc.vector.tensor_copy(picked[:], g_tab[0, t][:].indirect(idx[:]))
-            for first in range(0, S, HALF):
-                add_shape(0, t, first, picked[:, first : first + HALF])
-        for first in range(0, S, HALF):
-            quantise_h(0, first)
+            squared_separation(1, t, 0)
         for half in range(2):
-            for t in range(PACK):
-                squared_separation(1, t, half)
-
+            squared_separation(0, PACK - 1, half)
+        for t in range(PACK):
+            squared_separation(1, t, 1)
         wr_w = held("wr_w", [P, 2, N], U32)
         for a in range(2):
             deal_columns(nc.scalar.copy, wr_w[:, a, :], wr_raw[:, a, :])
+
+        for t in range(PACK - 1):
+            picked = g_picked[t % 2]
+            nc.vector.tensor_copy(picked[:], g_tab[0, t][:].indirect(idx[:]))
+            add_shape(0, t, 0, S, picked[:])
+        wr_s = held("wr_s", [P, N], U8)
+        deal_columns(nc.vector.tensor_copy, wr_s[:], wr_s_raw[:])
+        for half, picked in enumerate(half_picked[:2]):
+            first = half * HALF
+            nc.vector.tensor_copy(picked[:], g_tab[0, PACK - 1][:].indirect(list_cols(idx, first, HALF)))
+            add_shape(0, PACK - 1, first, HALF, picked[:])
+            quantise_h(0, first, HALF, g_picked[half])
 
         y_w = [held("y_w%d" % g, [P, S], U32) for g in range(2)]
         y_s = held("y_s", [P, S], U8)
         out_rows = out_0.rearrange("(g p t) j -> g p t j", p=P, t=PACK)
 
-        def make_h(first):
-            for t in range(PACK):
-                picked = g_picked[(first // CHUNK) % 2][:, t * CHUNK : (t + 1) * CHUNK]
-                nc.vector.tensor_copy(picked, g_tab[1, t][:].indirect(list_cols(idx, first, CHUNK)))
-                add_shape(1, t, first, picked)
-            quantise_h(1, first)
+        def pick_and_add(t, first, count, picked):
+            nc.vector.tensor_copy(picked, g_tab[1, t][:].indirect(list_cols(idx, first, count)))
+            add_shape(1, t, first, count, picked)
 
         def make_y(first):
             cols = slice(first, first + CHUNK)
@@ -257,22 +264,22 @@ def tile_list_multiquadric_deform_kernel(
                 y_bf = y_rounded.tile([P, CHUNK, PACK], BF16, name="y_bf", tag="y_bf", align_bytes=AL)
                 for part in range(0, CHUNK, YCOLS):
                     moving = slice(first + part, first + part + YCOLS)
-                    acc = y_psum.tile([P, PACK, YCOLS], F32, name="acc", tag="acc")
+                    acc = psum.tile([P, PACK, YCOLS], F32, name="acc", tag="bank")
                     for t in range(PACK):
                         rows = slice(g * GROUP + t * P, g * GROUP + (t + 1) * P)
                         for b in range(2):
                             nc.tensor.matmul_mx(
                                 out=acc[:, t, :], lhsT=wr_w[:, b, rows].bitcast(FP8X4),
-                                lhsT_scale=w_s[8 + 4 * b : P, rows],
+                                lhsT_scale=wr_s[4 * b : P, rows],
                                 rhs=h_w[b][:, moving].bitcast(FP8X4), rhs_scale=h_s[b][:, moving],
                                 start=(b == 0), stop=(b == 1),
                             )
                     nc.scalar.copy(out=y[:, g, :, part : part + YCOLS], in_=acc[:])
-                    if first == 0:
+                    if first < HALF:
                         nc.scalar.copy(
                             out=y_bf[:, part : part + YCOLS, :], in_=acc[:].rearrange("p t j -> p j t")
                         )
-                if first > 0:
+                if first >= HALF:
                     nc.vector.tensor_copy(
                         out=y_bf[:].rearrange("p (c i) t -> p c t i", i=4),
                         in_=y[:, g].rearrange("p t (c i) -> p c t i", i=4),
@@ -287,11 +294,20 @@ def tile_list_multiquadric_deform_kernel(
                     in_=y_w[g][:, cols].bitcast(I32),
                 )
 
-        make_h(0)
-        for first in range(0, S, CHUNK):
-            if first + CHUNK < S:
-                make_h(first + CHUNK)
-            make_y(first)
+        for t in range(PACK):
+            pick_and_add(t, 0, HALF, half_picked[(t + 2) % 3][:])
+        quantise_h(1, 0, CHUNK, half_picked[1])
+        quantise_h(1, CHUNK, CHUNK, half_picked[2])
+        make_y(0)
+        for t in range(PACK - 1):
+            pick_and_add(t, HALF, HALF, half_picked[t][:])
+        make_y(CHUNK)
+        for part in range(2):
+            first = HALF + part * CHUNK
+            pick_and_add(PACK - 1, first, CHUNK, half_picked[0][:, part * CHUNK : (part + 1) * CHUNK])
+            quantise_h(1, first, CHUNK, g_picked[part])
+        for part in range(2):
+            make_y(HALF + part * CHUNK)
 
         for q in range(4):
             nc.sync.dma_start(

@@ -46,12 +46,11 @@ def tile_list_multiquadric_deform_kernel(
         tab2_w = held("tab2_w", [P, T], U32)
         tab_s = held("tab_s", [P, T], U8)
         tab2_s = held("tab2_s", [P, T], U8)
-        wa_s_raw = held("wa_s_raw", [P, 2, H], U8)
-        wr_s_raw = held("wr_s_raw", [P, N], U8)
+        w_s_raw = held("w_s_raw", [P, 2, H], U8)
         v_s1 = held("v_s1", [P, S], U8)
         for plane in (tab_s, tab2_s):
             nc.gpsimd.memset(plane[:].bitcast(I32), 0)
-        for plane in (wa_s_raw, v_s1, wr_s_raw):
+        for plane in (w_s_raw, v_s1):
             nc.vector.memset(plane[:].bitcast(I32), 0)
 
         def load_scale_rows(queue, plane, scales):
@@ -105,7 +104,7 @@ def tile_list_multiquadric_deform_kernel(
         )
         for q in range(4):
             nc.sync.dma_start(
-                out=wa_s_raw[32 * q : 32 * q + 4].bitcast(I32),
+                out=w_s_raw[32 * q : 32 * q + 4].bitcast(I32),
                 in_=wa_scales[:, 4 * q : 4 * q + 4, :].rearrange("a r n -> r a n").bitcast(I32),
             )
 
@@ -113,6 +112,11 @@ def tile_list_multiquadric_deform_kernel(
         nc.vector.tensor_copy(v_s[:], tab_s[:].indirect(idx[:]))
         shift_planes(v_s1, v_s)
         load_wb(0)
+        for q in range(4):
+            nc.sync.dma_start(
+                out=w_s_raw[32 * q + 4 : 32 * q + 12, 0, :].bitcast(I32),
+                in_=wr_scales[:, 4 * q : 4 * q + 4, :].bitcast(I32),
+            )
         load_wb(1)
         load_g(0, 0)
         load_g(0, 1)
@@ -122,7 +126,6 @@ def tile_list_multiquadric_deform_kernel(
             in_=wr_words.rearrange("a p n i -> p a (n i)").bitcast(I32),
         )
         load_g(0, 2)
-        load_scale_rows(nc.sync, wr_s_raw, wr_scales)
         load_g(0, 3)
         for t in range(PACK):
             load_g(1, t)
@@ -130,7 +133,7 @@ def tile_list_multiquadric_deform_kernel(
         def list_cols(tile, first, count):
             return tile[:, first // 16 : (first + count) // 16]
 
-        g_picked = [held("g_picked%d" % i, [P, S], F32) for i in range(2)]
+        g_picked = [held("g_picked%d" % i, [P, S], F32) for i in range(3)]
 
         wa_w = held("wa_w", [P, 2, H], U16)
         for a in range(2):
@@ -138,7 +141,7 @@ def tile_list_multiquadric_deform_kernel(
 
         wb_w = [held("wb_w%d" % b, [P, GROUP], U32) for b in range(2)]
         wb_s = [held("wb_s%d" % b, [P, GROUP], U8) for b in range(2)]
-        half_picked = [held("half_picked%d" % i, [P, HALF], F32) for i in range(3)]
+        pair = [held("pair%d" % i, [P, 2 * CHUNK], F32) for i in range(2)]
 
         def quantise_wb(b, buffer):
             wb_bf = buffer[:].bitcast(BF16)
@@ -162,13 +165,13 @@ def tile_list_multiquadric_deform_kernel(
             nc.vector.tensor_copy(v_w[a][:], tab_w[a][:].indirect(idx[:]))
         nc.vector.tensor_copy(v2_s[:], tab2_s[:].indirect(idx2[:]))
         nc.vector.tensor_copy(v2_w[:], tab2_w[:].indirect(idx2[:]))
-        wa_s = held("wa_s", [P, 2, H], U8)
+        w_s = held("w_s", [P, 2, H], U8)
         nc.vector.tensor_copy(
-            out=wa_s[:].rearrange("p a (b t m) -> p (a b) m t", t=PACK, m=P),
-            in_=wa_s_raw[:].rearrange("p a (b m t) -> p (a b) m t", t=PACK, m=P),
+            out=w_s[:].rearrange("p a (b t m) -> p (a b) m t", t=PACK, m=P),
+            in_=w_s_raw[:].rearrange("p a (b m t) -> p (a b) m t", t=PACK, m=P),
         )
 
-        width = {0: S, 1: HALF}
+        width = {0: S, 1: CHUNK}
         x = {}
         for b in range(2):
             for first in range(0, S, width[b]):
@@ -183,11 +186,11 @@ def tile_list_multiquadric_deform_kernel(
             cols = slice(half * HALF, (half + 1) * HALF)
             d = psum.tile([P, HALF], F32, name="d", tag="bank")
             nc.tensor.matmul_mx(
-                out=d[:], lhsT=wa_w[:, 0, rows].bitcast(FP4X4), lhsT_scale=wa_s[:, 0, rows],
+                out=d[:], lhsT=wa_w[:, 0, rows].bitcast(FP4X4), lhsT_scale=w_s[:, 0, rows],
                 rhs=v_w[0][:, cols].bitcast(FP8X4), rhs_scale=v_s[:, cols], start=True, stop=False,
             )
             nc.tensor.matmul_mx(
-                out=d[:], lhsT=wa_w[:, 1, rows].bitcast(FP4X4), lhsT_scale=wa_s[:, 1, rows],
+                out=d[:], lhsT=wa_w[:, 1, rows].bitcast(FP4X4), lhsT_scale=w_s[:, 1, rows],
                 rhs=v_w[1][:, cols].bitcast(FP8X4), rhs_scale=v_s1[:, cols], start=False, stop=False,
             )
             nc.tensor.matmul_mx(
@@ -212,7 +215,7 @@ def tile_list_multiquadric_deform_kernel(
         h_s = [held("h_s%d" % b, [P, S], U8) for b in range(2)]
 
         def quantise_h(b, first, n, buffer):
-            h_bf = buffer[:, : 2 * n].bitcast(BF16)
+            h_bf = buffer.bitcast(BF16)
             nc.scalar.activation(
                 out=h_bf.rearrange("p (c i t) -> p c t i", i=4, t=PACK),
                 in_=x_cols(b, first, n).rearrange("p t (c i) -> p c t i", i=4),
@@ -238,16 +241,14 @@ def tile_list_multiquadric_deform_kernel(
             deal_columns(nc.scalar.copy, wr_w[:, a, :], wr_raw[:, a, :])
 
         for t in range(PACK - 1):
-            picked = g_picked[t % 2]
+            picked = g_picked[t]
             nc.vector.tensor_copy(picked[:], g_tab[0, t][:].indirect(idx[:]))
             add_shape(0, t, 0, S, picked[:])
-        wr_s = held("wr_s", [P, N], U8)
-        deal_columns(nc.vector.tensor_copy, wr_s[:], wr_s_raw[:])
-        for half, picked in enumerate(half_picked[:2]):
+        for half, picked in enumerate((pair[1], pair[0])):
             first = half * HALF
             nc.vector.tensor_copy(picked[:], g_tab[0, PACK - 1][:].indirect(list_cols(idx, first, HALF)))
             add_shape(0, PACK - 1, first, HALF, picked[:])
-            quantise_h(0, first, HALF, g_picked[half])
+            quantise_h(0, first, HALF, g_picked[half][:])
 
         y_w = [held("y_w%d" % g, [P, S], U32) for g in range(2)]
         y_s = held("y_s", [P, S], U8)
@@ -257,12 +258,27 @@ def tile_list_multiquadric_deform_kernel(
             nc.vector.tensor_copy(picked, g_tab[1, t][:].indirect(list_cols(idx, first, count)))
             add_shape(1, t, first, count, picked)
 
-        def make_y(first):
-            cols = slice(first, first + CHUNK)
-            y = stage.tile([P, 2, PACK, CHUNK], F32, name="y", tag="stage", align_bytes=AL)
+        def make_h(chunk):
+            first = chunk * CHUNK
+            last_chunk = first + CHUNK == S
+            for t in range(PACK):
+                buffer = pair[(chunk + 1 + t // 2) % 2]
+                picked = buffer[:, (t % 2) * CHUNK : (t % 2 + 1) * CHUNK]
+                if last_chunk and t == PACK - 1:
+                    for part in range(0, CHUNK, YCOLS):
+                        pick_and_add(t, first + part, YCOLS, picked[:, part : part + YCOLS])
+                        quantise_h(1, first + part, YCOLS, g_picked[part // YCOLS][:, : 2 * YCOLS])
+                else:
+                    pick_and_add(t, first, CHUNK, picked)
+            if not last_chunk:
+                quantise_h(1, first, CHUNK, pair[(chunk + 1) % 2][:])
+
+        def make_y(first, count):
+            cols = slice(first, first + count)
+            y = stage.tile([P, 2, PACK, count], F32, name="y", tag="stage", align_bytes=AL)
             for g in range(2):
-                y_bf = y_rounded.tile([P, CHUNK, PACK], BF16, name="y_bf", tag="y_bf", align_bytes=AL)
-                for part in range(0, CHUNK, YCOLS):
+                y_bf = y_rounded.tile([P, count, PACK], BF16, name="y_bf", tag="y_bf", align_bytes=AL)
+                for part in range(0, count, YCOLS):
                     moving = slice(first + part, first + part + YCOLS)
                     acc = psum.tile([P, PACK, YCOLS], F32, name="acc", tag="bank")
                     for t in range(PACK):
@@ -270,7 +286,7 @@ def tile_list_multiquadric_deform_kernel(
                         for b in range(2):
                             nc.tensor.matmul_mx(
                                 out=acc[:, t, :], lhsT=wr_w[:, b, rows].bitcast(FP8X4),
-                                lhsT_scale=wr_s[4 * b : P, rows],
+                                lhsT_scale=w_s[4 + 4 * b : P, 0, rows],
                                 rhs=h_w[b][:, moving].bitcast(FP8X4), rhs_scale=h_s[b][:, moving],
                                 start=(b == 0), stop=(b == 1),
                             )
@@ -294,20 +310,13 @@ def tile_list_multiquadric_deform_kernel(
                     in_=y_w[g][:, cols].bitcast(I32),
                 )
 
-        for t in range(PACK):
-            pick_and_add(t, 0, HALF, half_picked[(t + 2) % 3][:])
-        quantise_h(1, 0, CHUNK, half_picked[1])
-        quantise_h(1, CHUNK, CHUNK, half_picked[2])
-        make_y(0)
-        for t in range(PACK - 1):
-            pick_and_add(t, HALF, HALF, half_picked[t][:])
-        make_y(CHUNK)
-        for part in range(2):
-            first = HALF + part * CHUNK
-            pick_and_add(PACK - 1, first, CHUNK, half_picked[0][:, part * CHUNK : (part + 1) * CHUNK])
-            quantise_h(1, first, CHUNK, g_picked[part])
-        for part in range(2):
-            make_y(HALF + part * CHUNK)
+        chunks = S // CHUNK
+        make_h(0)
+        for chunk in range(chunks - 1):
+            make_h(chunk + 1)
+            make_y(chunk * CHUNK, CHUNK)
+        for first in range(S - CHUNK, S, YCOLS):
+            make_y(first, YCOLS)
 
         for q in range(4):
             nc.sync.dma_start(

@@ -240,86 +240,100 @@ def tile_list_multiquadric_deform_kernel(
         for a in range(2):
             deal_columns(nc.scalar.copy, wr_w[:, a, :], wr_raw[:, a, :])
 
-        for t in range(PACK - 1):
-            picked = g_picked[t]
-            nc.vector.tensor_copy(picked[:], g_tab[0, t][:].indirect(idx[:]))
-            add_shape(0, t, 0, S, picked[:])
-        for half, picked in enumerate((pair[1], pair[0])):
-            first = half * HALF
-            nc.vector.tensor_copy(picked[:], g_tab[0, PACK - 1][:].indirect(list_cols(idx, first, HALF)))
-            add_shape(0, PACK - 1, first, HALF, picked[:])
-            quantise_h(0, first, HALF, g_picked[half][:])
+        def pick(b, t, first, count, picked):
+            nc.vector.tensor_copy(picked, g_tab[b, t][:].indirect(list_cols(idx, first, count)))
 
-        y_w = [held("y_w%d" % g, [P, S], U32) for g in range(2)]
+        def pick_and_add(b, jobs):
+            for n in range(len(jobs) + 1):
+                if n < len(jobs):
+                    pick(b, *jobs[n])
+                if n > 0:
+                    add_shape(b, *jobs[n - 1])
+
+        pick_and_add(
+            0,
+            [(t, 0, S, g_picked[t][:]) for t in range(PACK - 1)]
+            + [(PACK - 1, half * HALF, HALF, pair[1 - half][:]) for half in range(2)],
+        )
+        for half in range(2):
+            quantise_h(0, half * HALF, HALF, g_picked[half][:])
+
+        y_w = held("y_w", [P, 2, S], U32)
         y_s = held("y_s", [P, S], U8)
         out_rows = out_0.rearrange("(g p t) j -> g p t j", p=P, t=PACK)
-
-        def pick_and_add(t, first, count, picked):
-            nc.vector.tensor_copy(picked, g_tab[1, t][:].indirect(list_cols(idx, first, count)))
-            add_shape(1, t, first, count, picked)
+        out_words = out_1.rearrange("g p n i -> p g (n i)").bitcast(I32)
 
         def make_h(chunk):
             first = chunk * CHUNK
-            last_chunk = first + CHUNK == S
+            jobs = []
             for t in range(PACK):
                 buffer = pair[(chunk + 1 + t // 2) % 2]
-                picked = buffer[:, (t % 2) * CHUNK : (t % 2 + 1) * CHUNK]
-                if last_chunk and t == PACK - 1:
-                    for part in range(0, CHUNK, YCOLS):
-                        pick_and_add(t, first + part, YCOLS, picked[:, part : part + YCOLS])
-                        quantise_h(1, first + part, YCOLS, g_picked[part // YCOLS][:, : 2 * YCOLS])
-                else:
-                    pick_and_add(t, first, CHUNK, picked)
-            if not last_chunk:
+                jobs.append((t, first, CHUNK, buffer[:, (t % 2) * CHUNK : (t % 2 + 1) * CHUNK]))
+            pick_and_add(1, jobs[:2])
+            if first + CHUNK < S:
+                pick_and_add(1, jobs[2:])
                 quantise_h(1, first, CHUNK, pair[(chunk + 1) % 2][:])
+            else:
+                t, first, count, picked = jobs[3]
+                parts = range(0, count, YCOLS)
+                pick_and_add(
+                    1, [jobs[2]] + [(t, first + part, YCOLS, picked[:, part : part + YCOLS]) for part in parts]
+                )
+                for part in parts:
+                    quantise_h(1, first + part, YCOLS, g_picked[part // YCOLS][:, : 2 * YCOLS])
 
-        def make_y(first, count):
+        y = {}
+
+        def make_y(first, count, g):
             cols = slice(first, first + count)
-            y = stage.tile([P, 2, PACK, count], F32, name="y", tag="stage", align_bytes=AL)
-            for g in range(2):
-                y_bf = y_rounded.tile([P, count, PACK], BF16, name="y_bf", tag="y_bf", align_bytes=AL)
-                for part in range(0, count, YCOLS):
-                    moving = slice(first + part, first + part + YCOLS)
-                    acc = psum.tile([P, PACK, YCOLS], F32, name="acc", tag="bank")
-                    for t in range(PACK):
-                        rows = slice(g * GROUP + t * P, g * GROUP + (t + 1) * P)
-                        for b in range(2):
-                            nc.tensor.matmul_mx(
-                                out=acc[:, t, :], lhsT=wr_w[:, b, rows].bitcast(FP8X4),
-                                lhsT_scale=w_s[4 + 4 * b : P, 0, rows],
-                                rhs=h_w[b][:, moving].bitcast(FP8X4), rhs_scale=h_s[b][:, moving],
-                                start=(b == 0), stop=(b == 1),
-                            )
-                    nc.scalar.copy(out=y[:, g, :, part : part + YCOLS], in_=acc[:])
-                    if first < HALF:
-                        nc.scalar.copy(
-                            out=y_bf[:, part : part + YCOLS, :], in_=acc[:].rearrange("p t j -> p j t")
+            if g == 0:
+                y[first] = stage.tile([P, 2, PACK, count], F32, name="y", tag="stage", align_bytes=AL)
+            y_rows = y[first][:, g]
+            y_bf = y_rounded.tile([P, count, PACK], BF16, name="y_bf", tag="y_bf", align_bytes=AL)
+            for part in range(0, count, YCOLS):
+                moving = slice(first + part, first + part + YCOLS)
+                acc = psum.tile([P, PACK, YCOLS], F32, name="acc", tag="bank")
+                for t in range(PACK):
+                    rows = slice(g * GROUP + t * P, g * GROUP + (t + 1) * P)
+                    for b in range(2):
+                        nc.tensor.matmul_mx(
+                            out=acc[:, t, :], lhsT=wr_w[:, b, rows].bitcast(FP8X4),
+                            lhsT_scale=w_s[4 + 4 * b : P, 0, rows],
+                            rhs=h_w[b][:, moving].bitcast(FP8X4), rhs_scale=h_s[b][:, moving],
+                            start=(b == 0), stop=(b == 1),
                         )
-                if first >= HALF:
-                    nc.vector.tensor_copy(
-                        out=y_bf[:].rearrange("p (c i) t -> p c t i", i=4),
-                        in_=y[:, g].rearrange("p t (c i) -> p c t i", i=4),
+                if count == YCOLS and g == 1:
+                    nc.vector.tensor_copy(out=y_rows[:, :, part : part + YCOLS], in_=acc[:])
+                else:
+                    nc.scalar.copy(out=y_rows[:, :, part : part + YCOLS], in_=acc[:])
+                if first == 0:
+                    nc.scalar.copy(
+                        out=y_bf[:, part : part + YCOLS, :], in_=acc[:].rearrange("p t j -> p j t")
                     )
-                nc.sync.dma_start(out=out_rows[g][:, :, cols], in_=y[:, g])
-                nc.vector.quantize_mx(
-                    out=y_w[g][:, cols].bitcast(FP8X4), scales=y_s[4 * g : P, cols],
-                    in_=y_bf[:].rearrange("p n t -> p (n t)"),
+            if first > 0:
+                nc.vector.tensor_copy(
+                    out=y_bf[:].rearrange("p (c i) t -> p c t i", i=4),
+                    in_=y_rows.rearrange("p t (c i) -> p c t i", i=4),
                 )
-                nc.sync.dma_start(
-                    out=out_1[g].rearrange("p n i -> p (n i)").bitcast(I32)[:, cols],
-                    in_=y_w[g][:, cols].bitcast(I32),
-                )
+            nc.sync.dma_start(out=out_rows[g][:, :, cols], in_=y_rows)
+            nc.vector.quantize_mx(
+                out=y_w[:, g, cols].bitcast(FP8X4), scales=y_s[4 * g : P, cols],
+                in_=y_bf[:].rearrange("p n t -> p (n t)"),
+            )
+            if g == 1:
+                nc.sync.dma_start(out=out_words[:, :, cols], in_=y_w[:, :, cols].bitcast(I32))
 
-        chunks = S // CHUNK
         make_h(0)
-        for chunk in range(chunks - 1):
+        for chunk in range(S // CHUNK - 1):
+            make_y(chunk * CHUNK, CHUNK, 0)
             make_h(chunk + 1)
-            make_y(chunk * CHUNK, CHUNK)
+            make_y(chunk * CHUNK, CHUNK, 1)
         for first in range(S - CHUNK, S, YCOLS):
-            make_y(first, YCOLS)
+            for g in range(2):
+                make_y(first, YCOLS, g)
 
         for q in range(4):
-            nc.sync.dma_start(
+            nc.scalar.dma_start(
                 out=out_2[:, 4 * q : 4 * q + 4, :].bitcast(I32),
                 in_=y_s[32 * q : 32 * q + 8, :].bitcast(I32),
             )

from contextlib import ExitStack

import concourse.mybir as mybir

K, K2, T, S, H, N = 1024, 512, 2048, 1024, 1024, 1024
FLOPS = 2 * S * (K * H + K2 * H + H * N)

F32 = mybir.dt.float32
BF16 = mybir.dt.bfloat16
I32 = mybir.dt.int32
U32 = mybir.dt.uint32
U16 = mybir.dt.uint16
U8 = mybir.dt.uint8
FP8X4 = mybir.dt.float8_e4m3fn_x4
FP4X4 = mybir.dt.float4_e2m1fn_x4
ACT = mybir.ActivationFunctionType
ALU = mybir.AluOpType

P = 128
PACK = 4
GROUP = P * PACK
HALF = 512
CHUNK = 256
YCOLS = 128
AL = 64


def tile_list_multiquadric_deform_kernel(
    tc, tab_words, tab_scales, tab2_words, tab2_scales, offs, offs2, gT,
    wa_words, wa_scales, wb, amp, wr_words, wr_scales, out_0, out_1, out_2,
):
    nc = tc.nc
    with ExitStack() as ctx:
        keep = ctx.enter_context(tc.tile_pool(name="keep", bufs=1))
        g_pool = ctx.enter_context(tc.tile_pool(name="g_rows", bufs=6))
        stage = ctx.enter_context(tc.tile_pool(name="stage", bufs=3))
        y_rounded = ctx.enter_context(tc.tile_pool(name="y_rounded", bufs=4))
        psum = ctx.enter_context(tc.psum_pool(name="psum", bufs=8))

        def held(name, shape, dtype):
            return keep.tile(shape, dtype, name=name, align_bytes=AL)

        idx = keep.tile([P, S // 16], U16, name="idx")
        idx2 = keep.tile([P, S // 16], U16, name="idx2")
        tab_w = [held("tab_w%d" % a, [P, T], U32) for a in range(2)]
        tab2_w = held("tab2_w", [P, T], U32)
        tab_s = held("tab_s", [P, T], U8)
        tab2_s = held("tab2_s", [P, T], U8)
        w_s_raw = held("w_s_raw", [P, 2, H], U8)
        v_s1 = held("v_s1", [P, S], U8)
        for plane in (tab_s, tab2_s):
            nc.gpsimd.memset(plane[:].bitcast(I32), 0)
        for plane in (w_s_raw, v_s1):
            nc.vector.memset(plane[:].bitcast(I32), 0)

        def load_scale_rows(queue, plane, scales):
            passes = scales.shape[0]
            for q in range(4):
                queue.dma_start(
                    out=plane[32 * q : 32 * q + 4 * passes, :].bitcast(I32),
                    in_=scales[:, 4 * q : 4 * q + 4, :].bitcast(I32),
                )

        def load_words(tile, words):
            nc.sync.dma_start(
                out=tile[:].bitcast(I32), in_=words.rearrange("p n i -> p (n i)").bitcast(I32)
            )

        def deal_columns(copy, dealt, raw):
            copy(
                out=dealt.rearrange("p (b t m) -> p b m t", t=PACK, m=P),
                in_=raw.rearrange("p (b m t) -> p b m t", t=PACK, m=P),
            )

        def shift_planes(second, both):
            nc.sync.dma_start(out=second[0:112, :].bitcast(I32), in_=both[4:116, :].bitcast(I32))

        wb_rows = wb.rearrange("(p i) r -> p i r", i=PACK)
        g_rows = gT.rearrange("(b p t) n -> b t p n", p=P, t=PACK)
        wb_raw = {}
        g_tab = {}

        def load_wb(b):
            wb_raw[b] = stage.tile([P, PACK, GROUP], F32, name="wb_raw%d" % b, tag="stage", align_bytes=AL)
            nc.sync.dma_start(out=wb_raw[b][:], in_=wb_rows[:, :, b * GROUP : (b + 1) * GROUP])

        def load_g(b, t):
            g_tab[b, t] = g_pool.tile([P, T], F32, name="g_tab%d%d" % (b, t), tag="g_tab", align_bytes=AL)
            nc.sync.dma_start(out=g_tab[b, t][:], in_=g_rows[b, t])

        nc.sync.dma_start(idx[:], offs)
        nc.sync.dma_start(idx2[:], offs2)
        amp_sb = held("amp_sb", [P, 2, PACK], F32)
        nc.sync.dma_start(out=amp_sb[:], in_=amp.rearrange("(b p t) -> p b t", p=P, t=PACK))
        load_scale_rows(nc.sync, tab_s, tab_scales)
        load_words(tab_w[0], tab_words[0])
        load_words(tab_w[1], tab_words[1])
        load_scale_rows(nc.sync, tab2_s, tab2_scales)
        load_words(tab2_w, tab2_words[0])
        wa_raw = held("wa_raw", [P, 2, H], U16)
        nc.sync.dma_start(
            out=wa_raw[:].bitcast(I32),
            in_=wa_words.rearrange("a p n -> p a n").bitcast(I32),
        )
        for q in range(4):
            nc.sync.dma_start(
                out=w_s_raw[32 * q : 32 * q + 4].bitcast(I32),
                in_=wa_scales[:, 4 * q : 4 * q + 4, :].rearrange("a r n -> r a n").bitcast(I32),
            )

        v_s = held("v_s", [P, S], U8)
        nc.vector.tensor_copy(v_s[:], tab_s[:].indirect(idx[:]))
        shift_planes(v_s1, v_s)
        load_wb(0)
        for q in range(4):
            nc.sync.dma_start(
                out=w_s_raw[32 * q + 4 : 32 * q + 12, 0, :].bitcast(I32),
                in_=wr_scales[:, 4 * q : 4 * q + 4, :].bitcast(I32),
            )
        load_wb(1)
        load_g(0, 0)
        load_g(0, 1)
        wr_raw = held("wr_raw", [P, 2, N], U32)
        nc.sync.dma_start(
            out=wr_raw[:].bitcast(I32),
            in_=wr_words.rearrange("a p n i -> p a (n i)").bitcast(I32),
        )
        load_g(0, 2)
        load_g(0, 3)
        for t in range(PACK):
            load_g(1, t)

        def list_cols(tile, first, count):
            return tile[:, first // 16 : (first + count) // 16]

        g_picked = [held("g_picked%d" % i, [P, S], F32) for i in range(3)]

        wa_w = held("wa_w", [P, 2, H], U16)
        for a in range(2):
            deal_columns(nc.scalar.copy, wa_w[:, a, :], wa_raw[:, a, :])

        wb_w = [held("wb_w%d" % b, [P, GROUP], U32) for b in range(2)]
        wb_s = [held("wb_s%d" % b, [P, GROUP], U8) for b in range(2)]
        pair = [held("pair%d" % i, [P, 2 * CHUNK], F32) for i in range(2)]

        def quantise_wb(b, buffer):
            wb_bf = buffer[:].bitcast(BF16)
            nc.scalar.activation(
                out=wb_bf.rearrange("p (t m i) -> p m i t", t=PACK, i=PACK),
                in_=wb_raw[b][:].rearrange("p i (m t) -> p m i t", t=PACK),
                func=ACT.Copy,
                scale=-1.0,
            )
            nc.vector.quantize_mx(out=wb_w[b][:].bitcast(FP8X4), scales=wb_s[b][:], in_=wb_bf)

        for b in range(2):
            quantise_wb(b, g_picked[1 - b])
        amp_sq = held("amp_sq", [P, 2, PACK], F32)
        nc.vector.tensor_tensor(out=amp_sq[:], in0=amp_sb[:], in1=amp_sb[:], op=ALU.mult)

        v_w = [held("v_w%d" % a, [P, S], U32) for a in range(2)]
        v2_w = held("v2_w", [P, S], U32)
        v2_s = held("v2_s", [P, S], U8)
        for a in range(2):
            nc.vector.tensor_copy(v_w[a][:], tab_w[a][:].indirect(idx[:]))
        nc.vector.tensor_copy(v2_s[:], tab2_s[:].indirect(idx2[:]))
        nc.vector.tensor_copy(v2_w[:], tab2_w[:].indirect(idx2[:]))
        w_s = held("w_s", [P, 2, H], U8)
        nc.vector.tensor_copy(
            out=w_s[:].rearrange("p a (b t m) -> p (a b) m t", t=PACK, m=P),
            in_=w_s_raw[:].rearrange("p a (b m t) -> p (a b) m t", t=PACK, m=P),
        )

        width = {0: S, 1: CHUNK}
        x = {}
        for b in range(2):
            for first in range(0, S, width[b]):
                x[b, first] = held("x%d_%d" % (b, first), [P, PACK, width[b]], F32)

        def x_cols(b, first, count):
            start = first - first % width[b]
            return x[b, start][:, :, first - start : first - start + count]

        def squared_separation(b, t, half):
            rows = slice(b * GROUP + t * P, b * GROUP + (t + 1) * P)
            cols = slice(half * HALF, (half + 1) * HALF)
            d = psum.tile([P, HALF], F32, name="d", tag="bank")
            nc.tensor.matmul_mx(
                out=d[:], lhsT=wa_w[:, 0, rows].bitcast(FP4X4), lhsT_scale=w_s[:, 0, rows],
                rhs=v_w[0][:, cols].bitcast(FP8X4), rhs_scale=v_s[:, cols], start=True, stop=False,
            )
            nc.tensor.matmul_mx(
                out=d[:], lhsT=wa_w[:, 1, rows].bitcast(FP4X4), lhsT_scale=w_s[:, 1, rows],
                rhs=v_w[1][:, cols].bitcast(FP8X4), rhs_scale=v_s1[:, cols], start=False, stop=False,
            )
            nc.tensor.matmul_mx(
                out=d[:], lhsT=wb_w[b][:, t * P : (t + 1) * P].bitcast(FP8X4), lhsT_scale=wb_s[b][:, t * P : (t + 1) * P],
                rhs=v2_w[:, cols].bitcast(FP8X4), rhs_scale=v2_s[:, cols], start=False, stop=True,
            )
            step = min(HALF, width[b])
            for part in range(0, HALF, step):
                nc.scalar.activation(
                    out=x_cols(b, half * HALF + part, step)[:, t, :], in_=d[:, part : part + step],
                    func=ACT.Square, scale=amp_sb[:, b, t : t + 1],
                )

        def add_shape(b, t, first, count, picked):
            squares = x_cols(b, first, count)[:, t, :]
            nc.vector.scalar_tensor_tensor(
                out=squares, in0=picked, scalar=amp_sq[:, b, t : t + 1],
                in1=squares, op0=ALU.mult, op1=ALU.add,
            )

        h_w = [held("h_w%d" % b, [P, S], U32) for b in range(2)]
        h_s = [held("h_s%d" % b, [P, S], U8) for b in range(2)]

        def quantise_h(b, first, n, buffer):
            h_bf = buffer.bitcast(BF16)
            nc.scalar.activation(
                out=h_bf.rearrange("p (c i t) -> p c t i", i=4, t=PACK),
                in_=x_cols(b, first, n).rearrange("p t (c i) -> p c t i", i=4),
                func=ACT.Sqrt,
            )
            cols = slice(first, first + n)
            nc.vector.quantize_mx(
                out=h_w[b][:, cols].bitcast(FP8X4), scales=h_s[b][:, cols],
                in_=h_bf,
            )

        for t in range(PACK - 1):
            for half in range(2):
                squared_separation(0, t, half)
        for t in range(PACK):
            squared_separation(1, t, 0)
        for half in range(2):
            squared_separation(0, PACK - 1, half)
        for t in range(PACK):
            squared_separation(1, t, 1)
        wr_w = held("wr_w", [P, 2, N], U32)
        for a in range(2):
            deal_columns(nc.scalar.copy, wr_w[:, a, :], wr_raw[:, a, :])

        def pick(b, t, first, count, picked):
            nc.vector.tensor_copy(picked, g_tab[b, t][:].indirect(list_cols(idx, first, count)))

        def pick_and_add(b, jobs):
            for n in range(len(jobs) + 1):
                if n < len(jobs):
                    pick(b, *jobs[n])
                if n > 0:
                    add_shape(b, *jobs[n - 1])

        pick_and_add(
            0,
            [(t, 0, S, g_picked[t][:]) for t in range(PACK - 1)]
            + [(PACK - 1, half * HALF, HALF, pair[1 - half][:]) for half in range(2)],
        )
        for half in range(2):
            quantise_h(0, half * HALF, HALF, g_picked[half][:])

        y_w = held("y_w", [P, 2, S], U32)
        y_s = held("y_s", [P, S], U8)
        out_rows = out_0.rearrange("(g p t) j -> g p t j", p=P, t=PACK)
        out_words = out_1.rearrange("g p n i -> p g (n i)").bitcast(I32)

        def make_h(chunk):
            first = chunk * CHUNK
            jobs = []
            for t in range(PACK):
                buffer = pair[(chunk + 1 + t // 2) % 2]
                jobs.append((t, first, CHUNK, buffer[:, (t % 2) * CHUNK : (t % 2 + 1) * CHUNK]))
            pick_and_add(1, jobs[:2])
            if first + CHUNK < S:
                pick_and_add(1, jobs[2:])
                quantise_h(1, first, CHUNK, pair[(chunk + 1) % 2][:])
            else:
                t, first, count, picked = jobs[3]
                parts = range(0, count, YCOLS)
                pick_and_add(
                    1, [jobs[2]] + [(t, first + part, YCOLS, picked[:, part : part + YCOLS]) for part in parts]
                )
                for part in parts:
                    quantise_h(1, first + part, YCOLS, g_picked[part // YCOLS][:, : 2 * YCOLS])

        y = {}

        def make_y(first, count, g):
            cols = slice(first, first + count)
            if g == 0:
                y[first] = stage.tile([P, 2, PACK, count], F32, name="y", tag="stage", align_bytes=AL)
            y_rows = y[first][:, g]
            y_bf = y_rounded.tile([P, count, PACK], BF16, name="y_bf", tag="y_bf", align_bytes=AL)
            for part in range(0, count, YCOLS):
                moving = slice(first + part, first + part + YCOLS)
                acc = psum.tile([P, PACK, YCOLS], F32, name="acc", tag="bank")
                for t in range(PACK):
                    rows = slice(g * GROUP + t * P, g * GROUP + (t + 1) * P)
                    for b in range(2):
                        nc.tensor.matmul_mx(
                            out=acc[:, t, :], lhsT=wr_w[:, b, rows].bitcast(FP8X4),
                            lhsT_scale=w_s[4 + 4 * b : P, 0, rows],
                            rhs=h_w[b][:, moving].bitcast(FP8X4), rhs_scale=h_s[b][:, moving],
                            start=(b == 0), stop=(b == 1),
                        )
                if count == YCOLS and g == 1:
                    nc.vector.tensor_copy(out=y_rows[:, :, part : part + YCOLS], in_=acc[:])
                else:
                    nc.scalar.copy(out=y_rows[:, :, part : part + YCOLS], in_=acc[:])
                if first == 0:
                    nc.scalar.copy(
                        out=y_bf[:, part : part + YCOLS, :], in_=acc[:].rearrange("p t j -> p j t")
                    )
            if first > 0:
                nc.vector.tensor_copy(
                    out=y_bf[:].rearrange("p (c i) t -> p c t i", i=4),
                    in_=y_rows.rearrange("p t (c i) -> p c t i", i=4),
                )
            nc.sync.dma_start(out=out_rows[g][:, :, cols], in_=y_rows)
            nc.vector.quantize_mx(
                out=y_w[:, g, cols].bitcast(FP8X4), scales=y_s[4 * g : P, cols],
                in_=y_bf[:].rearrange("p n t -> p (n t)"),
            )
            if g == 1:
                nc.sync.dma_start(out=out_words[:, :, cols], in_=y_w[:, :, cols].bitcast(I32))

        make_h(0)
        for chunk in range(S // CHUNK - 1):
            make_y(chunk * CHUNK, CHUNK, 0)
            make_h(chunk + 1)
            make_y(chunk * CHUNK, CHUNK, 1)
        for first in range(S - CHUNK, S, YCOLS):
            for g in range(2):
                make_y(first, YCOLS, g)

        for q in range(4):
            nc.scalar.dma_start(
                out=out_2[:, 4 * q : 4 * q + 4, :].bitcast(I32),
                in_=y_s[32 * q : 32 * q + 8, :].bitcast(I32),
            )
